import numpy as np, ml_dtypes
CORES = [3,5,19,21,35,37,51,53,67,69]
N = 10
import mx_ref
NC, G = 128, 4
C = np.float32(0.037)
BF = ml_dtypes.bfloat16
def cut(t, i, w=512):
    return t[:, w * i:w * i + w]
def tile(rs):
    return np.stack(rs, axis=2).reshape(128, -1).astype(BF)
def layer(w, X):
    out = []
    for i in range(G):
        for t in range(len(X)):
            p = mx_ref.matmul(mx_ref.quantize(cut(w, len(X) * i + t)), X[t])
            z = p if t == 0 else z + p
        out.append(z)
    return out
def masked(A, E):
    return [(e * (a > 0)) * C for a, e in zip(A, E)]
def setup_inputs(rng):
    def f(*shape):
        return mx_ref.flush((rng.standard_normal(shape, dtype=np.float32) * np.exp2(rng.integers(-2, 3, shape[:-1] + (1,)))).astype(BF))
    return {"x": f(N, 128, 512), "e": f(N, 128, 512), "a": f(N, 128, G * 512), "w": f(N, 128, 512), "v": f(N, 128, 4 * NC)}
def setup_inputs_blocks(rng):
    d = setup_inputs(rng)
    for k in ("x", "e", "a", "w", "v"): d[k] = mx_ref.spread(d[k], rng, 2)
    return d
def setup_inputs_wide(rng):
    d = setup_inputs(rng)
    for k in ("x", "e", "a", "w", "v"): d[k] = mx_ref.flush((d[k].astype(np.float32) * np.exp2(rng.integers(-6, 7, (N, 1, 1))).astype(np.float32)).astype(BF))
    return d
def setup_inputs_zeros(rng):
    d = setup_inputs(rng); v = d["x"].reshape(N, 128, -1, 4).copy()
    v[np.broadcast_to((rng.random((N, 1, v.shape[2], 1)) < 0.33), v.shape)] = 0
    d["x"] = v.reshape(d["x"].shape)
    return d
def reference(x, e, a, w, v):
    T = [mx_ref.quantize(tile(masked(layer(a[j], [mx_ref.quantize(x[j])]), layer(a[j], [mx_ref.quantize(e[j])])))) for j in range(N)]
    y = np.zeros((N, 128, N * 128), np.float32); z = np.zeros((N, 128, NC), np.float32)
    for r in range(N):
        qw = mx_ref.quantize(w[r]); qv = mx_ref.quantize(v[r])
        for j in range(N):
            y[r][:, 128 * j:128 * j + 128] = mx_ref.matmul(qw, T[j])
            p = mx_ref.matmul(T[j], qv)
            z[r] = p if j == 0 else z[r] + p
    return {"y": y, "z": z}

@@ -1,0 +1,198 @@
+from concourse.bass import DstId, RemoteDMATransfer
+from concourse.mybir import AluOpType, ActivationFunctionType, dt
+
+F32, BF16, CODES, PLANE = "float32", "bfloat16", "float8_e4m3fn_x4", "uint8"
+W = 128
+SCRATCH = {
+    "xb": ("sbuf", [128, 512], BF16), "eb": ("sbuf", [128, 512], BF16), "ab": ("sbuf", [128, 2048], BF16),
+    "wb": ("sbuf", [128, 512], BF16), "vb": ("sbuf", [128, 512], BF16),
+    "xc": ("sbuf", [128, W], CODES), "xs": ("sbuf", [128, W], PLANE),
+    "ec": ("sbuf", [128, W], CODES), "es": ("sbuf", [128, W], PLANE),
+    "ac": ("sbuf", [128, 4 * W], CODES), "as_": ("sbuf", [128, 4 * W], PLANE),
+    "wc": ("sbuf", [128, W], CODES), "ws": ("sbuf", [128, W], PLANE),
+    "vc": ("sbuf", [128, W], CODES), "vs": ("sbuf", [128, W], PLANE),
+    "mk": ("sbuf", [128, 512], F32),
+    "t": ("sbuf", [128, 512], BF16),
+    "tc": ("sbuf", [128, 10 * W], CODES),
+    "ts": ("sbuf", [128, 10 * W], PLANE),
+    "yo": ("sbuf", [128, 10 * W], F32), "zo": ("sbuf", [128, W], F32),
+    "p": ("psum", [128, 8 * 512], F32),
+}
+STEPS = 7
+SEMAPHORES = (["ld_x", "ld_e", "ld_a0", "ld_a2", "ld_a3", "ld_w", "ld_v", "q_x", "q_e", "q_t", "q_w", "q_v", "sent", "z_mm", "z_cp", "z_st", "y_st"]
+              + ["q_a%d" % i for i in range(4)] + ["u%d" % i for i in range(4)] + ["d%d" % i for i in range(4)]
+              + ["m%d" % i for i in range(4)] + ["r%d" % i for i in range(4)]
+              + ["t%d" % j for j in range(10)] + ["y_mm%d" % i for i in range(STEPS)] + ["y_cp%d" % i for i in range(STEPS)])
+
+
+def slot(k, p):
+    return p if k == 0 else 2 + 2 * p + (k - 1) if k <= 2 else 2 * k + p
+
+
+def rank_program(g, core, T, topo):
+    rank = T.rank_of(core)
+    if rank is None:
+        return
+    cores, S = T.cores, T.sem
+    chips = []
+    for c in cores:
+        if topo.chip(c) not in chips:
+            chips.append(topo.chip(c))
+    n = len(chips)
+    here = chips.index(topo.chip(core))
+
+    def on(k):
+        return [c for c in cores if topo.chip(c) == chips[(here + k) % n]]
+
+    def same(k):
+        return [c for c in on(k) if topo.die(c) == topo.die(core)][0]
+
+    def other(k):
+        return [c for c in on(k) if topo.die(c) != topo.die(core)][0]
+
+    def place(c):
+        return [q for q in cores if topo.chip(q) == topo.chip(c)].index(c)
+
+    mate = other(0)
+    me, him = place(core), place(mate)
+    far = topo.mask(core, same(1))
+    whole = topo.mask(core, mate)
+    near = whole & ~far
+
+    def bits(m):
+        return bin(m).count("1")
+
+    def codes(a, m=1):
+        return T.tc[:, W * a:W * (a + m)].bitcast(dt.uint8)
+
+    def plane(a, m=1):
+        return T.ts[:, W * a:W * (a + m)]
+
+    def dst(c):
+        rid, pid, _ = topo.addr(c)
+        return DstId(rid=rid, pnc=pid)
+
+    def sem(c):
+        return S["t%d" % T.rank_of(c)]
+
+    g.sync.dma_start(T.xb[:], T.x[:]).then_inc(S.ld_x, 16)
+    g.scalar.dma_start(T.eb[:], T.e[:]).then_inc(S.ld_e, 16)
+    g.sync.dma_start(T.ab[:, 0:1024], T.a[:, 0:1024]).then_inc(S.ld_a0, 16)
+    g.scalar.dma_start(T.ab[:, 1024:1536], T.a[:, 1024:1536]).then_inc(S.ld_a2, 16)
+    g.sync.dma_start(T.ab[:, 1536:2048], T.a[:, 1536:2048]).then_inc(S.ld_a3, 16)
+    g.sync.wait_ge(S.ld_a3, 16)
+    g.sync.dma_start(T.wb[:], T.w[:]).then_inc(S.ld_w, 16)
+    g.sync.dma_start(T.vb[:], T.v[:]).then_inc(S.ld_v, 16)
+
+    vec = g.vector
+
+    def quant(c, s, b, lo, hi, done):
+        vec.quantize_mx(c[:, lo:hi], s[:, lo:hi], b[:, 4 * lo:4 * hi]).then_inc(done, 1)
+
+    def fold(b):
+        cols = slice(128 * b, 128 * b + 128)
+        vec.wait_ge(S["u%d" % b], 1)
+        vec.tensor_scalar(T.mk[:, cols], T.p[:, 512 * b:512 * b + 128], 0.0, 0.037, AluOpType.is_gt, AluOpType.mult).then_inc(S["m%d" % b], 1)
+        vec.wait_ge(S["m%d" % b], 1)
+        vec.wait_ge(S["d%d" % b], 1)
+        vec.tensor_tensor(T.t[:, b:512:4], T.p[:, 2048 + 512 * b:2048 + 512 * b + 128], T.mk[:, cols], AluOpType.mult).then_inc(S["r%d" % b], 1)
+
+    vec.wait_ge(S.ld_x, 16)
+    quant(T.xc, T.xs, T.xb, 0, W, S.q_x)
+    vec.wait_ge(S.ld_e, 16)
+    quant(T.ec, T.es, T.eb, 0, W, S.q_e)
+    vec.wait_ge(S.ld_a0, 16)
+    quant(T.ac, T.as_, T.ab, 0, W, S.q_a0)
+    quant(T.ac, T.as_, T.ab, W, 2 * W, S.q_a1)
+    fold(0)
+    fold(1)
+    vec.wait_ge(S.ld_a2, 16)
+    quant(T.ac, T.as_, T.ab, 2 * W, 3 * W, S.q_a2)
+    fold(2)
+    vec.wait_ge(S.ld_a3, 16)
+    quant(T.ac, T.as_, T.ab, 3 * W, 4 * W, S.q_a3)
+    fold(3)
+    for b in range(4):
+        vec.wait_ge(S["r%d" % b], 1)
+    own = slot(0, me)
+    vec.quantize_mx(T.tc[:, W * own:W * own + W], T.ts[:, W * own:W * own + W], T.t[:]).then_inc(S.q_t, 1)
+    vec.wait_ge(S.ld_w, 16)
+    quant(T.wc, T.ws, T.wb, 0, W, S.q_w)
+    vec.wait_ge(S.ld_v, 16)
+    quant(T.vc, T.vs, T.vb, 0, W, S.q_v)
+
+    ten = g.tensor
+    ten.wait_ge(S.q_x, 1)
+    for b in range(4):
+        a, s = T.ac[:, W * b:W * b + W], T.as_[:, W * b:W * b + W]
+        ten.wait_ge(S["q_a%d" % b], 1)
+        ten.matmul_mx(T.p[:, 512 * b:512 * b + 128], a, s, T.xc[:], T.xs[:], True, True).then_inc(S["u%d" % b], 1)
+        if b == 0:
+            ten.wait_ge(S.q_e, 1)
+        ten.matmul_mx(T.p[:, 2048 + 512 * b:2048 + 512 * b + 128], a, s, T.ec[:], T.es[:], True, True).then_inc(S["d%d" % b], 1)
+
+    sent = [0]
+
+    def copy(routes):
+        for view in (codes, plane):
+            g.remote_dma_fused([RemoteDMATransfer(dst_ids=[dst(c) for c, _ in to], dma_engine_mask=m, remote_sem=sm,
+                                                  srcs=[view(a, w)], dsts=[view(q, w) for _, q in to])
+                                for a, w, m, sm, to in routes], local_sem=S.sent)
+            sent[0] += sum(bits(m) for _, _, m, _, _ in routes)
+
+    g.wait_ge(S.q_t, 1)
+    copy([(own, 1, far, sem(core), [(same(k), slot(k, me)) for k in (1, 2)]),
+          (own, 1, near, sem(core), [(mate, own)])])
+    copy([(own, 1, far, sem(core), [(same(3), slot(3, me)), (same(4), slot(4, me)), (other(4), slot(4, me))])])
+    s = [None] + [same(-k) for k in range(1, 5)]
+    o = [mate] + [other(-k) for k in range(1, 5)]
+    direct = 2 * bits(far)
+    for k in (1, 2):
+        g.wait_ge(sem(s[k]), direct)
+    copy([(slot(1, me), 2, near, sem(s[1]), [(mate, slot(1, me))])])
+    g.wait_ge(sem(s[3]), direct)
+    copy([(slot(3, me), 1, whole, sem(s[3]), [(mate, slot(3, me))])])
+
+    steps = [
+        ([(S.q_t, 1), (S.q_w, 1), (S.q_v, 1), (sem(mate), 2 * bits(near))], slot(0, 0), [on(0)[0], on(0)[1]]),
+        ([(sem(s[1]), direct), (sem(s[2]), direct)], slot(1, me), [s[1], s[2]]),
+        ([(sem(s[3]), direct)], slot(3, me), [s[3]]),
+        ([(sem(o[1]), 2 * bits(near))], slot(1, him), [o[1], o[2]]),
+        ([(sem(s[4]), direct)], slot(4, me), [s[4]]),
+        ([(sem(o[4]), direct)], slot(4, him), [o[4]]),
+        ([(sem(o[3]), 2 * bits(whole))], slot(3, him), [o[3]]),
+    ]
+    total, done = 10, 0
+    for i, (waits, a, tiles) in enumerate(steps):
+        for sm, v in waits:
+            ten.wait_ge(sm, v)
+        m = len(tiles)
+        ten.matmul_mx(T.p[:, 512 * i:512 * i + W * m], T.wc[:], T.ws[:], T.tc[:, W * a:W * (a + m)], T.ts[:, W * a:W * (a + m)],
+                      True, True).then_inc(S["y_mm%d" % i], 1)
+        for q in range(a, a + m):
+            mm = ten.matmul_mx(T.p[:, 512 * 7:512 * 7 + W], T.tc[:, W * q:W * q + W], T.ts[:, W * q:W * q + W], T.vc[:], T.vs[:],
+                               done == 0, done == total - 1)
+            done += 1
+            if done == total:
+                mm.then_inc(S.z_mm, 1)
+        runs = []
+        for k, c in enumerate(tiles):
+            r = T.rank_of(c)
+            if runs and runs[-1][0] + runs[-1][2] == r:
+                runs[-1][2] += 1
+            else:
+                runs.append([r, k, 1])
+        vec.wait_ge(S["y_mm%d" % i], 1)
+        for r, k, w in runs:
+            vec.tensor_copy(T.yo[:, W * r:W * (r + w)], T.p[:, 512 * i + W * k:512 * i + W * (k + w)]).then_inc(S["y_cp%d" % i], 1)
+        g.sync.wait_ge(S["y_cp%d" % i], len(runs))
+        for r, k, w in runs:
+            g.sync.dma_start(T.y[:, W * r:W * (r + w)], T.yo[:, W * r:W * (r + w)]).then_inc(S.y_st, 16)
+        done_dmas = runs if i == 0 else done_dmas + runs
+    g.scalar.wait_ge(S.z_mm, 1)
+    g.scalar.activation(T.zo[:], T.p[:, 512 * 7:512 * 7 + W], ActivationFunctionType.Copy).then_inc(S.z_cp, 1)
+    g.scalar.wait_ge(S.z_cp, 1)
+    g.scalar.dma_start(T.z[:], T.zo[:]).then_inc(S.z_st, 16)
+    g.scalar.wait_ge(S.z_st, 16)
+    g.sync.wait_ge(S.y_st, 16 * len(done_dmas))
+    g.wait_ge(S.sent, sent[0])

@@ -3,6 +3,12 @@ from concourse.mybir import AluOpType, ActivationFunctionType, dt
 
 F32, BF16, CODES, PLANE = "float32", "bfloat16", "float8_e4m3fn_x4", "uint8"
 W = 128
+SENDS = [[("far", [("s", 1), ("s", 2)])],
+         [("far", [("s", 3), ("s", 4), ("o", 4)])],
+         [("near", [("o", 0)])]]
+FORWARDS = [((1, 2), "near"), ((3,), "whole")]
+ARRIVALS = [[("s", 1), ("s", 2)], [("s", 3)], [("o", 1), ("o", 2)], [("s", 4)], [("o", 4)], [("o", 3)]]
+
 SCRATCH = {
     "xb": ("sbuf", [128, 512], BF16), "eb": ("sbuf", [128, 512], BF16), "ab": ("sbuf", [128, 2048], BF16),
     "wb": ("sbuf", [128, 512], BF16), "vb": ("sbuf", [128, 512], BF16),
@@ -18,15 +24,14 @@ SCRATCH = {
     "yo": ("sbuf", [128, 10 * W], F32), "zo": ("sbuf", [128, W], F32),
     "p": ("psum", [128, 8 * 512], F32),
 }
-STEPS = 7
 SEMAPHORES = (["ld_x", "ld_e", "ld_a0", "ld_a2", "ld_a3", "ld_w", "ld_v", "q_x", "q_e", "q_t", "q_w", "q_v", "sent", "z_mm", "z_cp", "z_st", "y_st"]
               + ["q_a%d" % i for i in range(4)] + ["u%d" % i for i in range(4)] + ["d%d" % i for i in range(4)]
               + ["m%d" % i for i in range(4)] + ["r%d" % i for i in range(4)]
-              + ["t%d" % j for j in range(10)] + ["y_mm%d" % i for i in range(STEPS)] + ["y_cp%d" % i for i in range(STEPS)])
+              + ["t%d" % j for j in range(10)] + ["y_mm%d" % i for i in range(7)] + ["y_cp%d" % i for i in range(7)])
 
 
 def slot(k, p):
-    return p if k == 0 else 2 + 2 * p + (k - 1) if k <= 2 else 2 * k + p
+    return p if k == 0 else 2 + 4 * ((k - 1) // 2) + 2 * p + (k - 1) % 2
 
 
 def rank_program(g, core, T, topo):
@@ -41,26 +46,18 @@ def rank_program(g, core, T, topo):
     n = len(chips)
     here = chips.index(topo.chip(core))
 
-    def on(k):
-        return [c for c in cores if topo.chip(c) == chips[(here + k) % n]]
-
-    def same(k):
-        return [c for c in on(k) if topo.die(c) == topo.die(core)][0]
-
-    def other(k):
-        return [c for c in on(k) if topo.die(c) != topo.die(core)][0]
+    def at(side, k):
+        return [c for c in cores if topo.chip(c) == chips[(here + k) % n] and (topo.die(c) == topo.die(core)) == (side == "s")][0]
 
     def place(c):
         return [q for q in cores if topo.chip(q) == topo.chip(c)].index(c)
 
-    mate = other(0)
-    me, him = place(core), place(mate)
-    far = topo.mask(core, same(1))
+    mate = at("o", 0)
+    me = place(core)
+    own = slot(0, me)
+    far = topo.mask(core, at("s", 1))
     whole = topo.mask(core, mate)
-    near = whole & ~far
-
-    def bits(m):
-        return bin(m).count("1")
+    masks = {"far": far, "whole": whole, "near": whole & ~far}
 
     def codes(a, m=1):
         return T.tc[:, W * a:W * (a + m)].bitcast(dt.uint8)
@@ -75,6 +72,9 @@ def rank_program(g, core, T, topo):
     def sem(c):
         return S["t%d" % T.rank_of(c)]
 
+    def bits(m):
+        return bin(m).count("1")
+
     g.sync.dma_start(T.xb[:], T.x[:]).then_inc(S.ld_x, 16)
     g.scalar.dma_start(T.eb[:], T.e[:]).then_inc(S.ld_e, 16)
     g.sync.dma_start(T.ab[:, 0:1024], T.a[:, 0:1024]).then_inc(S.ld_a0, 16)
@@ -86,40 +86,42 @@ def rank_program(g, core, T, topo):
 
     vec = g.vector
 
-    def quant(c, s, b, lo, hi, done):
+    def quant(c, s, b, i, load, done):
+        if load is not None:
+            vec.wait_ge(load, 16)
+        lo, hi = W * i, W * i + W
         vec.quantize_mx(c[:, lo:hi], s[:, lo:hi], b[:, 4 * lo:4 * hi]).then_inc(done, 1)
 
-    def fold(b):
-        cols = slice(128 * b, 128 * b + 128)
+    def mask(b):
         vec.wait_ge(S["u%d" % b], 1)
-        vec.tensor_scalar(T.mk[:, cols], T.p[:, 512 * b:512 * b + 128], 0.0, 0.037, AluOpType.is_gt, AluOpType.mult).then_inc(S["m%d" % b], 1)
-        vec.wait_ge(S["m%d" % b], 1)
-        vec.wait_ge(S["d%d" % b], 1)
-        vec.tensor_tensor(T.t[:, b:512:4], T.p[:, 2048 + 512 * b:2048 + 512 * b + 128], T.mk[:, cols], AluOpType.mult).then_inc(S["r%d" % b], 1)
+        vec.tensor_scalar(T.mk[:, 128 * b:128 * b + 128], T.p[:, 512 * b:512 * b + 128], 0.0, 0.037, AluOpType.is_gt,
+                          AluOpType.mult).then_inc(S["m%d" % b], 1)
 
-    vec.wait_ge(S.ld_x, 16)
-    quant(T.xc, T.xs, T.xb, 0, W, S.q_x)
-    vec.wait_ge(S.ld_e, 16)
-    quant(T.ec, T.es, T.eb, 0, W, S.q_e)
-    vec.wait_ge(S.ld_a0, 16)
-    quant(T.ac, T.as_, T.ab, 0, W, S.q_a0)
-    quant(T.ac, T.as_, T.ab, W, 2 * W, S.q_a1)
-    fold(0)
-    fold(1)
-    vec.wait_ge(S.ld_a2, 16)
-    quant(T.ac, T.as_, T.ab, 2 * W, 3 * W, S.q_a2)
-    fold(2)
-    vec.wait_ge(S.ld_a3, 16)
-    quant(T.ac, T.as_, T.ab, 3 * W, 4 * W, S.q_a3)
-    fold(3)
+    def mult(b):
+        vec.wait_ge(S["d%d" % b], 1)
+        vec.wait_ge(S["m%d" % b], 1)
+        vec.tensor_tensor(T.t[:, b:512:4], T.p[:, 2048 + 512 * b:2048 + 512 * b + 128], T.mk[:, 128 * b:128 * b + 128],
+                          AluOpType.mult).then_inc(S["r%d" % b], 1)
+
+    quant(T.xc, T.xs, T.xb, 0, S.ld_x, S.q_x)
+    quant(T.ec, T.es, T.eb, 0, S.ld_e, S.q_e)
+    quant(T.ac, T.as_, T.ab, 0, S.ld_a0, S.q_a0)
+    quant(T.ac, T.as_, T.ab, 1, None, S.q_a1)
+    mask(0)
+    mask(1)
+    mult(0)
+    mult(1)
+    quant(T.ac, T.as_, T.ab, 2, S.ld_a2, S.q_a2)
+    mask(2)
+    quant(T.ac, T.as_, T.ab, 3, S.ld_a3, S.q_a3)
+    mult(2)
+    mask(3)
+    mult(3)
     for b in range(4):
         vec.wait_ge(S["r%d" % b], 1)
-    own = slot(0, me)
     vec.quantize_mx(T.tc[:, W * own:W * own + W], T.ts[:, W * own:W * own + W], T.t[:]).then_inc(S.q_t, 1)
-    vec.wait_ge(S.ld_w, 16)
-    quant(T.wc, T.ws, T.wb, 0, W, S.q_w)
-    vec.wait_ge(S.ld_v, 16)
-    quant(T.vc, T.vs, T.vb, 0, W, S.q_v)
+    quant(T.wc, T.ws, T.wb, 0, S.ld_w, S.q_w)
+    quant(T.vc, T.vs, T.vb, 0, S.ld_v, S.q_v)
 
     ten = g.tensor
     ten.wait_ge(S.q_x, 1)
@@ -132,6 +134,7 @@ def rank_program(g, core, T, topo):
         ten.matmul_mx(T.p[:, 2048 + 512 * b:2048 + 512 * b + 128], a, s, T.ec[:], T.es[:], True, True).then_inc(S["d%d" % b], 1)
 
     sent = [0]
+    arrive = {}
 
     def copy(routes):
         for view in (codes, plane):
@@ -141,32 +144,29 @@ def rank_program(g, core, T, topo):
             sent[0] += sum(bits(m) for _, _, m, _, _ in routes)
 
     g.wait_ge(S.q_t, 1)
-    copy([(own, 1, far, sem(core), [(same(k), slot(k, me)) for k in (1, 2)]),
-          (own, 1, near, sem(core), [(mate, own)])])
-    copy([(own, 1, far, sem(core), [(same(3), slot(3, me)), (same(4), slot(4, me)), (other(4), slot(4, me))])])
-    s = [None] + [same(-k) for k in range(1, 5)]
-    o = [mate] + [other(-k) for k in range(1, 5)]
-    direct = 2 * bits(far)
-    for k in (1, 2):
-        g.wait_ge(sem(s[k]), direct)
-    copy([(slot(1, me), 2, near, sem(s[1]), [(mate, slot(1, me))])])
-    g.wait_ge(sem(s[3]), direct)
-    copy([(slot(3, me), 1, whole, sem(s[3]), [(mate, slot(3, me))])])
+    for call in SENDS:
+        copy([(own, 1, masks[m], sem(core), [(at(*t), slot(t[1], me)) for t in to]) for m, to in call])
+        for m, to in call:
+            for side, k in to:
+                arrive[(side, k)] = (sem(at(side, -k)), 2 * bits(masks[m]))
+    for ks, m in FORWARDS:
+        for k in ks:
+            g.wait_ge(*arrive[("s", k)])
+            arrive[("o", k)] = (sem(at("o", -ks[0])), 2 * bits(masks[m]))
+        q = slot(ks[0], me)
+        copy([(q, len(ks), masks[m], sem(at("s", -ks[0])), [(mate, q)])])
 
-    steps = [
-        ([(S.q_t, 1), (S.q_w, 1), (S.q_v, 1), (sem(mate), 2 * bits(near))], slot(0, 0), [on(0)[0], on(0)[1]]),
-        ([(sem(s[1]), direct), (sem(s[2]), direct)], slot(1, me), [s[1], s[2]]),
-        ([(sem(s[3]), direct)], slot(3, me), [s[3]]),
-        ([(sem(o[1]), 2 * bits(near))], slot(1, him), [o[1], o[2]]),
-        ([(sem(s[4]), direct)], slot(4, me), [s[4]]),
-        ([(sem(o[4]), direct)], slot(4, him), [o[4]]),
-        ([(sem(o[3]), 2 * bits(whole))], slot(3, him), [o[3]]),
-    ]
-    total, done = 10, 0
-    for i, (waits, a, tiles) in enumerate(steps):
+    total, done, stores = 10, 0, 0
+    for i, tiles in enumerate([None] + ARRIVALS):
+        if tiles is None:
+            waits, a, makers = [(S.q_t, 1), (S.q_w, 1), (S.q_v, 1), arrive[("o", 0)]], 0, sorted([core, mate], key=place)
+        else:
+            waits = [arrive[t] for t in tiles]
+            makers = [at(side, -k) for side, k in tiles]
+            a = slot(tiles[0][1], place(makers[0]))
         for sm, v in waits:
             ten.wait_ge(sm, v)
-        m = len(tiles)
+        m = len(makers)
         ten.matmul_mx(T.p[:, 512 * i:512 * i + W * m], T.wc[:], T.ws[:], T.tc[:, W * a:W * (a + m)], T.ts[:, W * a:W * (a + m)],
                       True, True).then_inc(S["y_mm%d" % i], 1)
         for q in range(a, a + m):
@@ -176,7 +176,7 @@ def rank_program(g, core, T, topo):
             if done == total:
                 mm.then_inc(S.z_mm, 1)
         runs = []
-        for k, c in enumerate(tiles):
+        for k, c in enumerate(makers):
             r = T.rank_of(c)
             if runs and runs[-1][0] + runs[-1][2] == r:
                 runs[-1][2] += 1
@@ -188,11 +188,11 @@ def rank_program(g, core, T, topo):
         g.sync.wait_ge(S["y_cp%d" % i], len(runs))
         for r, k, w in runs:
             g.sync.dma_start(T.y[:, W * r:W * (r + w)], T.yo[:, W * r:W * (r + w)]).then_inc(S.y_st, 16)
-        done_dmas = runs if i == 0 else done_dmas + runs
+            stores += 16
     g.scalar.wait_ge(S.z_mm, 1)
     g.scalar.activation(T.zo[:], T.p[:, 512 * 7:512 * 7 + W], ActivationFunctionType.Copy).then_inc(S.z_cp, 1)
     g.scalar.wait_ge(S.z_cp, 1)
     g.scalar.dma_start(T.z[:], T.zo[:]).then_inc(S.z_st, 16)
     g.scalar.wait_ge(S.z_st, 16)
-    g.sync.wait_ge(S.y_st, 16 * len(done_dmas))
+    g.sync.wait_ge(S.y_st, stores)
     g.wait_ge(S.sent, sent[0])

@@ -3,11 +3,15 @@ from concourse.mybir import AluOpType, ActivationFunctionType, dt
 
 F32, BF16, CODES, PLANE = "float32", "bfloat16", "float8_e4m3fn_x4", "uint8"
 W = 128
-SENDS = [[("far", [("s", 1), ("s", 2)])],
-         [("far", [("s", 3), ("s", 4), ("o", 4)])],
-         [("near", [("o", 0)])]]
-FORWARDS = [((1, 2), "near"), ((3,), "whole")]
-ARRIVALS = [[("s", 1), ("s", 2)], [("s", 3)], [("o", 1), ("o", 2)], [("s", 4)], [("o", 4)], [("o", 3)]]
+MATE = ("near", [("o", 0)])
+SENDS = [("codes", [("far", [("s", 1), ("s", 2)])]),
+         ("plane", [("far", [("s", 1), ("s", 2), ("s", 3), ("s", 4), ("o", 4)])]),
+         ("codes", [("far", [("s", 3), ("s", 4), ("o", 4)]), MATE]),
+         ("plane", [MATE])]
+FORWARDS = [("codes", (1, 2), "near"), ("plane", (1, 2, 3), "near"), ("codes", (3,), "whole")]
+STEPS = [([("s", 1), ("s", 2)], ("scalar", "sync")), ([("o", 0)], ("sync",)), ([("s", 3)], ("scalar",)),
+         ([("o", 1), ("o", 2)], ("sync", "scalar")), ([("s", 4)], ("sync",)), ([("o", 4)], ("scalar",)), ([("o", 3)], ("sync",))]
+ON_SCALAR = (5,)
 
 SCRATCH = {
     "xb": ("sbuf", [128, 512], BF16), "eb": ("sbuf", [128, 512], BF16), "ab": ("sbuf", [128, 2048], BF16),
@@ -24,14 +28,16 @@ SCRATCH = {
     "yo": ("sbuf", [128, 10 * W], F32), "zo": ("sbuf", [128, W], F32),
     "p": ("psum", [128, 8 * 512], F32),
 }
-SEMAPHORES = (["ld_x", "ld_e", "ld_a0", "ld_a2", "ld_a3", "ld_w", "ld_v", "q_x", "q_e", "q_t", "q_w", "q_v", "sent", "z_mm", "z_cp", "z_st", "y_st"]
+SEMAPHORES = (["ld_x", "ld_e", "ld_a0", "ld_a2", "ld_w", "ld_v", "q_x", "q_e", "q_t", "q_w", "q_v", "r", "sent", "passed",
+               "z_mm", "z_cp", "st_sync", "st_scalar"]
               + ["q_a%d" % i for i in range(4)] + ["u%d" % i for i in range(4)] + ["d%d" % i for i in range(4)]
-              + ["m%d" % i for i in range(4)] + ["r%d" % i for i in range(4)]
-              + ["t%d" % j for j in range(10)] + ["y_mm%d" % i for i in range(7)] + ["y_cp%d" % i for i in range(7)])
+              + ["m%d" % i for i in range(4)]
+              + ["codes%d" % j for j in range(10)] + ["plane%d" % j for j in range(10)]
+              + ["y_mm%d" % i for i in range(7)] + ["y_cp%d" % i for i in range(7)])
 
 
 def slot(k, p):
-    return p if k == 0 else 2 + 4 * ((k - 1) // 2) + 2 * p + (k - 1) % 2
+    return p if k == 0 else 8 + p if k == 4 else 2 + 3 * p + (k - 1)
 
 
 def rank_program(g, core, T, topo):
@@ -59,18 +65,17 @@ def rank_program(g, core, T, topo):
     whole = topo.mask(core, mate)
     masks = {"far": far, "whole": whole, "near": whole & ~far}
 
-    def codes(a, m=1):
-        return T.tc[:, W * a:W * (a + m)].bitcast(dt.uint8)
-
-    def plane(a, m=1):
+    def view(kind, a, m=1):
+        if kind == "codes":
+            return T.tc[:, W * a:W * (a + m)].bitcast(dt.uint8)
         return T.ts[:, W * a:W * (a + m)]
 
     def dst(c):
         rid, pid, _ = topo.addr(c)
         return DstId(rid=rid, pnc=pid)
 
-    def sem(c):
-        return S["t%d" % T.rank_of(c)]
+    def sem(kind, c):
+        return S["%s%d" % (kind, T.rank_of(c))]
 
     def bits(m):
         return bin(m).count("1")
@@ -78,11 +83,11 @@ def rank_program(g, core, T, topo):
     g.sync.dma_start(T.xb[:], T.x[:]).then_inc(S.ld_x, 16)
     g.scalar.dma_start(T.eb[:], T.e[:]).then_inc(S.ld_e, 16)
     g.sync.dma_start(T.ab[:, 0:1024], T.a[:, 0:1024]).then_inc(S.ld_a0, 16)
-    g.scalar.dma_start(T.ab[:, 1024:1536], T.a[:, 1024:1536]).then_inc(S.ld_a2, 16)
-    g.sync.dma_start(T.ab[:, 1536:2048], T.a[:, 1536:2048]).then_inc(S.ld_a3, 16)
-    g.sync.wait_ge(S.ld_a3, 16)
+    g.scalar.dma_start(T.ab[:, 1024:2048], T.a[:, 1024:2048]).then_inc(S.ld_a2, 16)
+    g.sync.wait_ge(S.ld_a2, 16)
     g.sync.dma_start(T.wb[:], T.w[:]).then_inc(S.ld_w, 16)
-    g.sync.dma_start(T.vb[:], T.v[:]).then_inc(S.ld_v, 16)
+    g.scalar.wait_ge(S.ld_a2, 16)
+    g.scalar.dma_start(T.vb[:], T.v[:]).then_inc(S.ld_v, 16)
 
     vec = g.vector
 
@@ -101,7 +106,7 @@ def rank_program(g, core, T, topo):
         vec.wait_ge(S["d%d" % b], 1)
         vec.wait_ge(S["m%d" % b], 1)
         vec.tensor_tensor(T.t[:, b:512:4], T.p[:, 2048 + 512 * b:2048 + 512 * b + 128], T.mk[:, 128 * b:128 * b + 128],
-                          AluOpType.mult).then_inc(S["r%d" % b], 1)
+                          AluOpType.mult).then_inc(S.r, 1)
 
     quant(T.xc, T.xs, T.xb, 0, S.ld_x, S.q_x)
     quant(T.ec, T.es, T.eb, 0, S.ld_e, S.q_e)
@@ -112,13 +117,12 @@ def rank_program(g, core, T, topo):
     mult(0)
     mult(1)
     quant(T.ac, T.as_, T.ab, 2, S.ld_a2, S.q_a2)
+    quant(T.ac, T.as_, T.ab, 3, None, S.q_a3)
     mask(2)
-    quant(T.ac, T.as_, T.ab, 3, S.ld_a3, S.q_a3)
-    mult(2)
     mask(3)
+    mult(2)
     mult(3)
-    for b in range(4):
-        vec.wait_ge(S["r%d" % b], 1)
+    vec.wait_ge(S.r, 4)
     vec.quantize_mx(T.tc[:, W * own:W * own + W], T.ts[:, W * own:W * own + W], T.t[:]).then_inc(S.q_t, 1)
     quant(T.wc, T.ws, T.wb, 0, S.ld_w, S.q_w)
     quant(T.vc, T.vs, T.vb, 0, S.ld_v, S.q_v)
@@ -133,37 +137,41 @@ def rank_program(g, core, T, topo):
             ten.wait_ge(S.q_e, 1)
         ten.matmul_mx(T.p[:, 2048 + 512 * b:2048 + 512 * b + 128], a, s, T.ec[:], T.es[:], True, True).then_inc(S["d%d" % b], 1)
 
-    sent = [0]
+    count = {"sent": 0, "passed": 0}
     arrive = {}
 
-    def copy(routes):
-        for view in (codes, plane):
-            g.remote_dma_fused([RemoteDMATransfer(dst_ids=[dst(c) for c, _ in to], dma_engine_mask=m, remote_sem=sm,
-                                                  srcs=[view(a, w)], dsts=[view(q, w) for _, q in to])
-                                for a, w, m, sm, to in routes], local_sem=S.sent)
-            sent[0] += sum(bits(m) for _, _, m, _, _ in routes)
+    def call(kind, routes, local):
+        g.remote_dma_fused([RemoteDMATransfer(dst_ids=[dst(c) for c, _ in to], dma_engine_mask=m, remote_sem=sm,
+                                              srcs=[view(kind, a, w)], dsts=[view(kind, q, w) for _, q in to])
+                            for a, w, m, sm, to in routes], local_sem=S[local])
+        count[local] += sum(bits(m) for _, _, m, _, _ in routes)
 
     g.wait_ge(S.q_t, 1)
-    for call in SENDS:
-        copy([(own, 1, masks[m], sem(core), [(at(*t), slot(t[1], me)) for t in to]) for m, to in call])
-        for m, to in call:
+    for kind, routes in SENDS:
+        call(kind, [(own, 1, masks[m], sem(kind, core), [(at(*t), slot(t[1], me)) for t in to]) for m, to in routes], "sent")
+        for m, to in routes:
             for side, k in to:
-                arrive[(side, k)] = (sem(at(side, -k)), 2 * bits(masks[m]))
-    for ks, m in FORWARDS:
+                arrive[(kind, side, k)] = (sem(kind, at(side, -k)), bits(masks[m]))
+    for kind, ks, m in FORWARDS:
         for k in ks:
-            g.wait_ge(*arrive[("s", k)])
-            arrive[("o", k)] = (sem(at("o", -ks[0])), 2 * bits(masks[m]))
+            g.wait_ge(*arrive[(kind, "s", k)])
+            arrive[(kind, "o", k)] = (sem(kind, at("o", -ks[0])), bits(masks[m]))
         q = slot(ks[0], me)
-        copy([(q, len(ks), masks[m], sem(at("s", -ks[0])), [(mate, q)])])
+        call(kind, [(q, len(ks), masks[m], sem(kind, at("s", -ks[0])), [(mate, q)])], "passed")
 
-    total, done, stores = 10, 0, 0
-    for i, tiles in enumerate([None] + ARRIVALS):
-        if tiles is None:
-            waits, a, makers = [(S.q_t, 1), (S.q_w, 1), (S.q_v, 1), arrive[("o", 0)]], 0, sorted([core, mate], key=place)
-        else:
-            waits = [arrive[t] for t in tiles]
-            makers = [at(side, -k) for side, k in tiles]
-            a = slot(tiles[0][1], place(makers[0]))
+    queues = {"sync": g.sync, "scalar": g.scalar}
+    for q in queues.values():
+        q.wait_ge(S.sent, count["sent"])
+    total, done = 10, 0
+    stores = {"sync": 0, "scalar": 0}
+    for i, (tiles, by) in enumerate(STEPS):
+        makers = [at(side, -k) for side, k in tiles]
+        a = slot(tiles[0][1], place(makers[0]))
+        waits = [arrive[(kind,) + t] for t in tiles for kind in ("plane", "codes")]
+        if tiles == [("o", 0)]:
+            makers, a = sorted([core, mate], key=place), 0
+        if i == 0:
+            waits = [(S.q_t, 1), (S.q_w, 1), (S.q_v, 1)] + waits
         for sm, v in waits:
             ten.wait_ge(sm, v)
         m = len(makers)
@@ -182,17 +190,21 @@ def rank_program(g, core, T, topo):
                 runs[-1][2] += 1
             else:
                 runs.append([r, k, 1])
-        vec.wait_ge(S["y_mm%d" % i], 1)
+        scalar = i in ON_SCALAR
+        engine = g.scalar if scalar else vec
+        engine.wait_ge(S["y_mm%d" % i], 1)
         for r, k, w in runs:
-            vec.tensor_copy(T.yo[:, W * r:W * (r + w)], T.p[:, 512 * i + W * k:512 * i + W * (k + w)]).then_inc(S["y_cp%d" % i], 1)
-        g.sync.wait_ge(S["y_cp%d" % i], len(runs))
-        for r, k, w in runs:
-            g.sync.dma_start(T.y[:, W * r:W * (r + w)], T.yo[:, W * r:W * (r + w)]).then_inc(S.y_st, 16)
-            stores += 16
+            to, src = T.yo[:, W * r:W * (r + w)], T.p[:, 512 * i + W * k:512 * i + W * (k + w)]
+            (g.scalar.activation(to, src, ActivationFunctionType.Copy) if scalar else vec.tensor_copy(to, src)).then_inc(S["y_cp%d" % i], 1)
+        for k, (r, _, w) in enumerate(runs):
+            q = by[k % len(by)]
+            queues[q].wait_ge(S["y_cp%d" % i], len(runs))
+            queues[q].dma_start(T.y[:, W * r:W * (r + w)], T.yo[:, W * r:W * (r + w)]).then_inc(S["st_" + q], 16)
+            stores[q] += 16
     g.scalar.wait_ge(S.z_mm, 1)
     g.scalar.activation(T.zo[:], T.p[:, 512 * 7:512 * 7 + W], ActivationFunctionType.Copy).then_inc(S.z_cp, 1)
     g.scalar.wait_ge(S.z_cp, 1)
-    g.scalar.dma_start(T.z[:], T.zo[:]).then_inc(S.z_st, 16)
-    g.scalar.wait_ge(S.z_st, 16)
-    g.sync.wait_ge(S.y_st, stores)
-    g.wait_ge(S.sent, sent[0])
+    g.scalar.dma_start(T.z[:], T.zo[:]).then_inc(S.st_scalar, 16)
+    for q in queues:
+        queues[q].wait_ge(S["st_" + q], stores[q] + (16 if q == "scalar" else 0))
+    g.wait_ge(S.passed, count["passed"])

@@ -9,9 +9,15 @@ SENDS = [("codes", [("far", [("s", 1), ("s", 2)])]),
          ("codes", [("far", [("s", 3), ("s", 4), ("o", 4)]), MATE]),
          ("plane", [MATE])]
 FORWARDS = [("codes", (1, 2), "near"), ("plane", (1, 2, 3), "near"), ("codes", (3,), "whole")]
-STEPS = [([("s", 1), ("s", 2)], ("scalar", "sync")), ([("o", 0)], ("sync",)), ([("s", 3)], ("scalar",)),
-         ([("o", 1), ("o", 2)], ("sync", "scalar")), ([("s", 4)], ("sync",)), ([("o", 4)], ("scalar",)), ([("o", 3)], ("sync",))]
-ON_SCALAR = (5,)
+STORE_AFTER = 1
+STEPS = [(("s", 0), None), (("s", 1), "scalar"), (("o", 0), "sync"), (("s", 2), "scalar"), (("s", 3), "sync"),
+         (("s", 4), "scalar"), (("o", 1), "sync"), (("o", 4), "scalar"), (("o", 2), "sync"), (("o", 3), "sync")]
+ON_SCALAR = (7,)
+BANKS = 7
+LOADS = [("sync", "x", 0), ("scalar", "e", 0), ("sync", "a", 0), ("scalar", "a", 1), ("sync", "a", 2), ("scalar", "a", 3)]
+VECTOR = ["qx", "qe", "qa0", "qa1", "qa2", "qa3", "m2", "p0", "p2", "m3", "p1", "p3"]
+TENSOR = ["u0", "d0", "u1", "u2", "d1", "d2", "u3", "d3"]
+SCALAR = ["s0", "s1", "r0", "r1"]
 
 SCRATCH = {
     "xb": ("sbuf", [128, 512], BF16), "eb": ("sbuf", [128, 512], BF16), "ab": ("sbuf", [128, 2048], BF16),
@@ -21,6 +27,7 @@ SCRATCH = {
     "ac": ("sbuf", [128, 4 * W], CODES), "as_": ("sbuf", [128, 4 * W], PLANE),
     "wc": ("sbuf", [128, W], CODES), "ws": ("sbuf", [128, W], PLANE),
     "vc": ("sbuf", [128, W], CODES), "vs": ("sbuf", [128, W], PLANE),
+    "sg": ("sbuf", [128, 512], F32),
     "mk": ("sbuf", [128, 512], F32),
     "t": ("sbuf", [128, 512], BF16),
     "tc": ("sbuf", [128, 10 * W], CODES),
@@ -28,12 +35,10 @@ SCRATCH = {
     "yo": ("sbuf", [128, 10 * W], F32), "zo": ("sbuf", [128, W], F32),
     "p": ("psum", [128, 8 * 512], F32),
 }
-SEMAPHORES = (["ld_x", "ld_e", "ld_a0", "ld_a2", "ld_w", "ld_v", "q_x", "q_e", "q_t", "q_w", "q_v", "r", "sent", "passed",
+SEMAPHORES = (["ld_x0", "ld_e0", "ld_w", "ld_v", "q_x", "q_e", "q_t", "q_w", "q_v", "r", "sent", "passed", "go",
                "z_mm", "z_cp", "st_sync", "st_scalar"]
-              + ["q_a%d" % i for i in range(4)] + ["u%d" % i for i in range(4)] + ["d%d" % i for i in range(4)]
-              + ["m%d" % i for i in range(4)]
-              + ["codes%d" % j for j in range(10)] + ["plane%d" % j for j in range(10)]
-              + ["y_mm%d" % i for i in range(7)] + ["y_cp%d" % i for i in range(7)])
+              + [s + str(i) for s in ("ld_a", "q_a", "u", "d", "s", "m") for i in range(4)]
+              + [s + str(i) for s in ("codes", "plane", "y_mm", "y_cp") for i in range(10)])
 
 
 def slot(k, p):
@@ -64,6 +69,7 @@ def rank_program(g, core, T, topo):
     far = topo.mask(core, at("s", 1))
     whole = topo.mask(core, mate)
     masks = {"far": far, "whole": whole, "near": whole & ~far}
+    queues = {"sync": g.sync, "scalar": g.scalar}
 
     def view(kind, a, m=1):
         if kind == "codes":
@@ -80,65 +86,63 @@ def rank_program(g, core, T, topo):
     def bits(m):
         return bin(m).count("1")
 
-    g.sync.dma_start(T.xb[:], T.x[:]).then_inc(S.ld_x, 16)
-    g.scalar.dma_start(T.eb[:], T.e[:]).then_inc(S.ld_e, 16)
-    g.sync.dma_start(T.ab[:, 0:1024], T.a[:, 0:1024]).then_inc(S.ld_a0, 16)
-    g.scalar.dma_start(T.ab[:, 1024:2048], T.a[:, 1024:2048]).then_inc(S.ld_a2, 16)
-    g.sync.wait_ge(S.ld_a2, 16)
+    for q, name, i in LOADS:
+        lo, hi = 512 * i, 512 * i + 512
+        queues[q].dma_start(T[name + "b"][:, lo:hi], T[name][:, lo:hi]).then_inc(S["ld_%s%d" % (name, i)], 16)
+    g.sync.wait_ge(S.ld_a3, 16)
     g.sync.dma_start(T.wb[:], T.w[:]).then_inc(S.ld_w, 16)
-    g.scalar.wait_ge(S.ld_a2, 16)
-    g.scalar.dma_start(T.vb[:], T.v[:]).then_inc(S.ld_v, 16)
+    g.sync.dma_start(T.vb[:], T.v[:]).then_inc(S.ld_v, 16)
 
-    vec = g.vector
+    vec, ten = g.vector, g.tensor
 
     def quant(c, s, b, i, load, done):
-        if load is not None:
-            vec.wait_ge(load, 16)
+        vec.wait_ge(load, 16)
         lo, hi = W * i, W * i + W
         vec.quantize_mx(c[:, lo:hi], s[:, lo:hi], b[:, 4 * lo:4 * hi]).then_inc(done, 1)
 
-    def mask(b):
-        vec.wait_ge(S["u%d" % b], 1)
-        vec.tensor_scalar(T.mk[:, 128 * b:128 * b + 128], T.p[:, 512 * b:512 * b + 128], 0.0, 0.037, AluOpType.is_gt,
-                          AluOpType.mult).then_inc(S["m%d" % b], 1)
-
-    def mult(b):
-        vec.wait_ge(S["d%d" % b], 1)
-        vec.wait_ge(S["m%d" % b], 1)
-        vec.tensor_tensor(T.t[:, b:512:4], T.p[:, 2048 + 512 * b:2048 + 512 * b + 128], T.mk[:, 128 * b:128 * b + 128],
-                          AluOpType.mult).then_inc(S.r, 1)
-
-    quant(T.xc, T.xs, T.xb, 0, S.ld_x, S.q_x)
-    quant(T.ec, T.es, T.eb, 0, S.ld_e, S.q_e)
-    quant(T.ac, T.as_, T.ab, 0, S.ld_a0, S.q_a0)
-    quant(T.ac, T.as_, T.ab, 1, None, S.q_a1)
-    mask(0)
-    mask(1)
-    mult(0)
-    mult(1)
-    quant(T.ac, T.as_, T.ab, 2, S.ld_a2, S.q_a2)
-    quant(T.ac, T.as_, T.ab, 3, None, S.q_a3)
-    mask(2)
-    mask(3)
-    mult(2)
-    mult(3)
+    for step in VECTOR:
+        b = int(step[-1]) if step[-1] in "0123" else 0
+        lo, hi = 128 * b, 128 * b + 128
+        if step == "qx":
+            quant(T.xc, T.xs, T.xb, 0, S.ld_x0, S.q_x)
+        elif step == "qe":
+            quant(T.ec, T.es, T.eb, 0, S.ld_e0, S.q_e)
+        elif step[0] == "q":
+            quant(T.ac, T.as_, T.ab, b, S["ld_a%d" % b], S["q_a%d" % b])
+        elif step[0] == "m":
+            vec.wait_ge(S["u%d" % b], 1)
+            vec.tensor_scalar(T.mk[:, lo:hi], T.p[:, 512 * b:512 * b + 128], 0.0, 0.037, AluOpType.is_gt,
+                              AluOpType.mult).then_inc(S["m%d" % b], 1)
+        else:
+            vec.wait_ge(S["d%d" % b], 1)
+            vec.wait_ge(S["m%d" % b], 1)
+            vec.tensor_tensor(T.t[:, b:512:4], T.p[:, 2048 + 512 * b:2048 + 512 * b + 128], T.mk[:, lo:hi],
+                              AluOpType.mult).then_inc(S.r, 1)
     vec.wait_ge(S.r, 4)
     vec.quantize_mx(T.tc[:, W * own:W * own + W], T.ts[:, W * own:W * own + W], T.t[:]).then_inc(S.q_t, 1)
     quant(T.wc, T.ws, T.wb, 0, S.ld_w, S.q_w)
     quant(T.vc, T.vs, T.vb, 0, S.ld_v, S.q_v)
 
-    ten = g.tensor
-    ten.wait_ge(S.q_x, 1)
-    for b in range(4):
-        a, s = T.ac[:, W * b:W * b + W], T.as_[:, W * b:W * b + W]
+    for step in SCALAR:
+        b = int(step[1])
+        lo, hi = 128 * b, 128 * b + 128
+        if step[0] == "s":
+            g.scalar.wait_ge(S["u%d" % b], 1)
+            g.scalar.activation(T.sg[:, lo:hi], T.p[:, 512 * b:512 * b + 128], ActivationFunctionType.Sign).then_inc(S["s%d" % b], 1)
+        else:
+            g.scalar.wait_ge(S["s%d" % b], 1)
+            g.scalar.activation(T.mk[:, lo:hi], T.sg[:, lo:hi], ActivationFunctionType.Relu, scale=0.037).then_inc(S["m%d" % b], 1)
+
+    for step in TENSOR:
+        b = int(step[1])
+        bank, c, s, first = (0, T.xc, T.xs, S.q_x) if step[0] == "u" else (4, T.ec, T.es, S.q_e)
+        ten.wait_ge(first, 1)
         ten.wait_ge(S["q_a%d" % b], 1)
-        ten.matmul_mx(T.p[:, 512 * b:512 * b + 128], a, s, T.xc[:], T.xs[:], True, True).then_inc(S["u%d" % b], 1)
-        if b == 0:
-            ten.wait_ge(S.q_e, 1)
-        ten.matmul_mx(T.p[:, 2048 + 512 * b:2048 + 512 * b + 128], a, s, T.ec[:], T.es[:], True, True).then_inc(S["d%d" % b], 1)
+        ten.matmul_mx(T.p[:, 512 * (bank + b):512 * (bank + b) + 128], T.ac[:, W * b:W * b + W], T.as_[:, W * b:W * b + W],
+                      c[:], s[:], True, True).then_inc(S[step], 1)
 
     count = {"sent": 0, "passed": 0}
-    arrive = {}
+    arrive = {("codes", "s", 0): (S.q_t, 1), ("plane", "s", 0): (S.q_t, 1)}
 
     def call(kind, routes, local):
         g.remote_dma_fused([RemoteDMATransfer(dst_ids=[dst(c) for c, _ in to], dma_engine_mask=m, remote_sem=sm,
@@ -152,59 +156,54 @@ def rank_program(g, core, T, topo):
         for m, to in routes:
             for side, k in to:
                 arrive[(kind, side, k)] = (sem(kind, at(side, -k)), bits(masks[m]))
-    for kind, ks, m in FORWARDS:
+    for i, (kind, ks, m) in enumerate(FORWARDS):
+        if i == STORE_AFTER:
+            g.sem_inc(S.go, 1)
         for k in ks:
             g.wait_ge(*arrive[(kind, "s", k)])
             arrive[(kind, "o", k)] = (sem(kind, at("o", -ks[0])), bits(masks[m]))
         q = slot(ks[0], me)
         call(kind, [(q, len(ks), masks[m], sem(kind, at("s", -ks[0])), [(mate, q)])], "passed")
 
-    queues = {"sync": g.sync, "scalar": g.scalar}
     for q in queues.values():
-        q.wait_ge(S.sent, count["sent"])
-    total, done = 10, 0
+        q.wait_ge(S.go, 1)
     stores = {"sync": 0, "scalar": 0}
-    for i, (tiles, by) in enumerate(STEPS):
-        makers = [at(side, -k) for side, k in tiles]
-        a = slot(tiles[0][1], place(makers[0]))
-        waits = [arrive[(kind,) + t] for t in tiles for kind in ("plane", "codes")]
-        if tiles == [("o", 0)]:
-            makers, a = sorted([core, mate], key=place), 0
-        if i == 0:
-            waits = [(S.q_t, 1), (S.q_w, 1), (S.q_v, 1)] + waits
-        for sm, v in waits:
-            ten.wait_ge(sm, v)
-        m = len(makers)
-        ten.matmul_mx(T.p[:, 512 * i:512 * i + W * m], T.wc[:], T.ws[:], T.tc[:, W * a:W * (a + m)], T.ts[:, W * a:W * (a + m)],
-                      True, True).then_inc(S["y_mm%d" % i], 1)
-        for q in range(a, a + m):
-            mm = ten.matmul_mx(T.p[:, 512 * 7:512 * 7 + W], T.tc[:, W * q:W * q + W], T.ts[:, W * q:W * q + W], T.vc[:], T.vs[:],
-                               done == 0, done == total - 1)
-            done += 1
-            if done == total:
-                mm.then_inc(S.z_mm, 1)
-        runs = []
-        for k, c in enumerate(makers):
-            r = T.rank_of(c)
-            if runs and runs[-1][0] + runs[-1][2] == r:
-                runs[-1][2] += 1
-            else:
-                runs.append([r, k, 1])
-        scalar = i in ON_SCALAR
-        engine = g.scalar if scalar else vec
-        engine.wait_ge(S["y_mm%d" % i], 1)
-        for r, k, w in runs:
-            to, src = T.yo[:, W * r:W * (r + w)], T.p[:, 512 * i + W * k:512 * i + W * (k + w)]
-            (g.scalar.activation(to, src, ActivationFunctionType.Copy) if scalar else vec.tensor_copy(to, src)).then_inc(S["y_cp%d" % i], 1)
-        for k, (r, _, w) in enumerate(runs):
-            q = by[k % len(by)]
-            queues[q].wait_ge(S["y_cp%d" % i], len(runs))
-            queues[q].dma_start(T.y[:, W * r:W * (r + w)], T.yo[:, W * r:W * (r + w)]).then_inc(S["st_" + q], 16)
-            stores[q] += 16
+    z = T.p[:, 512 * BANKS:512 * BANKS + W]
+    ten.wait_ge(S.q_w, 1)
+    ten.wait_ge(S.q_v, 1)
+    for i, ((side, k), queue) in enumerate(STEPS):
+        maker = at(side, -k)
+        r, a, bank = T.rank_of(maker), slot(k, place(maker)), 512 * (i % BANKS)
+        codes, plane = T.tc[:, W * a:W * a + W], T.ts[:, W * a:W * a + W]
+        ten.wait_ge(*arrive[("plane", side, k)])
+        ten.wait_ge(*arrive[("codes", side, k)])
+        if i >= BANKS:
+            ten.wait_ge(S["y_cp%d" % (i - BANKS)], 1)
+        ten.matmul_mx(T.p[:, bank:bank + W], T.wc[:], T.ws[:], codes, plane, True, True).then_inc(S["y_mm%d" % i], 1)
+        mm = ten.matmul_mx(z, codes, plane, T.vc[:], T.vs[:], i == 0, i == len(STEPS) - 1)
+        if i == len(STEPS) - 1:
+            mm.then_inc(S.z_mm, 1)
+        out, src = T.yo[:, W * r:W * r + W], T.p[:, bank:bank + W]
+        if i in ON_SCALAR:
+            g.scalar.wait_ge(S["y_mm%d" % i], 1)
+            g.scalar.activation(out, src, ActivationFunctionType.Copy).then_inc(S["y_cp%d" % i], 1)
+        else:
+            vec.wait_ge(S["y_mm%d" % i], 1)
+            vec.tensor_copy(out, src).then_inc(S["y_cp%d" % i], 1)
+        if queue:
+            queues[queue].wait_ge(S["y_cp%d" % i], 1)
+            lo, hi = W * r, W * r + W
+            if maker == mate:
+                queues[queue].wait_ge(S.y_cp0, 1)
+                lo = W * min(r, rank)
+                hi = lo + 2 * W
+            queues[queue].dma_start(T.y[:, lo:hi], T.yo[:, lo:hi]).then_inc(S["st_" + queue], 16)
+            stores[queue] += 16
     g.scalar.wait_ge(S.z_mm, 1)
-    g.scalar.activation(T.zo[:], T.p[:, 512 * 7:512 * 7 + W], ActivationFunctionType.Copy).then_inc(S.z_cp, 1)
+    g.scalar.activation(T.zo[:], z, ActivationFunctionType.Copy).then_inc(S.z_cp, 1)
     g.scalar.wait_ge(S.z_cp, 1)
     g.scalar.dma_start(T.z[:], T.zo[:]).then_inc(S.st_scalar, 16)
     for q in queues:
         queues[q].wait_ge(S["st_" + q], stores[q] + (16 if q == "scalar" else 0))
+    g.wait_ge(S.sent, count["sent"])
     g.wait_ge(S.passed, count["passed"])

from concourse.bass import DstId, RemoteDMATransfer
from concourse.mybir import AluOpType, ActivationFunctionType, dt

F32, BF16, CODES, PLANE = "float32", "bfloat16", "float8_e4m3fn_x4", "uint8"
W = 128
MATE = ("near", [("o", 0)])
SENDS = [("codes", [("far", [("s", 1), ("s", 2)])]),
         ("plane", [("far", [("s", 1), ("s", 2), ("s", 3), ("s", 4), ("o", 4)])]),
         ("codes", [("far", [("s", 3), ("s", 4), ("o", 4)]), MATE]),
         ("plane", [MATE])]
FORWARDS = [("codes", (1, 2), "near"), ("plane", (1, 2, 3), "near"), ("codes", (3,), "whole")]
STORE_AFTER = 1
STEPS = [(("s", 0), None), (("s", 1), "scalar"), (("o", 0), "sync"), (("s", 2), "scalar"), (("s", 3), "sync"),
         (("s", 4), "scalar"), (("o", 1), "sync"), (("o", 4), "scalar"), (("o", 2), "sync"), (("o", 3), "sync")]
ON_SCALAR = (7,)
BANKS = 7
LOADS = [("sync", "x", 0), ("scalar", "e", 0), ("sync", "a", 0), ("scalar", "a", 1), ("sync", "a", 2), ("scalar", "a", 3)]
VECTOR = ["qx", "qe", "qa0", "qa1", "qa2", "qa3", "m2", "p0", "p2", "m3", "p1", "p3"]
TENSOR = ["u0", "d0", "u1", "u2", "d1", "d2", "u3", "d3"]
SCALAR = ["s0", "s1", "r0", "r1"]

SCRATCH = {
    "xb": ("sbuf", [128, 512], BF16), "eb": ("sbuf", [128, 512], BF16), "ab": ("sbuf", [128, 2048], BF16),
    "wb": ("sbuf", [128, 512], BF16), "vb": ("sbuf", [128, 512], BF16),
    "xc": ("sbuf", [128, W], CODES), "xs": ("sbuf", [128, W], PLANE),
    "ec": ("sbuf", [128, W], CODES), "es": ("sbuf", [128, W], PLANE),
    "ac": ("sbuf", [128, 4 * W], CODES), "as_": ("sbuf", [128, 4 * W], PLANE),
    "wc": ("sbuf", [128, W], CODES), "ws": ("sbuf", [128, W], PLANE),
    "vc": ("sbuf", [128, W], CODES), "vs": ("sbuf", [128, W], PLANE),
    "sg": ("sbuf", [128, 512], F32),
    "mk": ("sbuf", [128, 512], F32),
    "t": ("sbuf", [128, 512], BF16),
    "tc": ("sbuf", [128, 10 * W], CODES),
    "ts": ("sbuf", [128, 10 * W], PLANE),
    "yo": ("sbuf", [128, 10 * W], F32), "zo": ("sbuf", [128, W], F32),
    "p": ("psum", [128, 8 * 512], F32),
}
SEMAPHORES = (["ld_x0", "ld_e0", "ld_w", "ld_v", "q_x", "q_e", "q_t", "q_w", "q_v", "r", "sent", "passed", "go",
               "z_mm", "z_cp", "st_sync", "st_scalar"]
              + [s + str(i) for s in ("ld_a", "q_a", "u", "d", "s", "m") for i in range(4)]
              + [s + str(i) for s in ("codes", "plane", "y_mm", "y_cp") for i in range(10)])


def slot(k, p):
    return p if k == 0 else 8 + p if k == 4 else 2 + 3 * p + (k - 1)


def rank_program(g, core, T, topo):
    rank = T.rank_of(core)
    if rank is None:
        return
    cores, S = T.cores, T.sem
    chips = []
    for c in cores:
        if topo.chip(c) not in chips:
            chips.append(topo.chip(c))
    n = len(chips)
    here = chips.index(topo.chip(core))

    def at(side, k):
        return [c for c in cores if topo.chip(c) == chips[(here + k) % n] and (topo.die(c) == topo.die(core)) == (side == "s")][0]

    def place(c):
        return [q for q in cores if topo.chip(q) == topo.chip(c)].index(c)

    mate = at("o", 0)
    me = place(core)
    own = slot(0, me)
    far = topo.mask(core, at("s", 1))
    whole = topo.mask(core, mate)
    masks = {"far": far, "whole": whole, "near": whole & ~far}
    queues = {"sync": g.sync, "scalar": g.scalar}

    def view(kind, a, m=1):
        if kind == "codes":
            return T.tc[:, W * a:W * (a + m)].bitcast(dt.uint8)
        return T.ts[:, W * a:W * (a + m)]

    def dst(c):
        rid, pid, _ = topo.addr(c)
        return DstId(rid=rid, pnc=pid)

    def sem(kind, c):
        return S["%s%d" % (kind, T.rank_of(c))]

    def bits(m):
        return bin(m).count("1")

    for q, name, i in LOADS:
        lo, hi = 512 * i, 512 * i + 512
        queues[q].dma_start(T[name + "b"][:, lo:hi], T[name][:, lo:hi]).then_inc(S["ld_%s%d" % (name, i)], 16)
    g.sync.wait_ge(S.ld_a3, 16)
    g.sync.dma_start(T.wb[:], T.w[:]).then_inc(S.ld_w, 16)
    g.sync.dma_start(T.vb[:], T.v[:]).then_inc(S.ld_v, 16)

    vec, ten = g.vector, g.tensor

    def quant(c, s, b, i, load, done):
        vec.wait_ge(load, 16)
        lo, hi = W * i, W * i + W
        vec.quantize_mx(c[:, lo:hi], s[:, lo:hi], b[:, 4 * lo:4 * hi]).then_inc(done, 1)

    for step in VECTOR:
        b = int(step[-1]) if step[-1] in "0123" else 0
        lo, hi = 128 * b, 128 * b + 128
        if step == "qx":
            quant(T.xc, T.xs, T.xb, 0, S.ld_x0, S.q_x)
        elif step == "qe":
            quant(T.ec, T.es, T.eb, 0, S.ld_e0, S.q_e)
        elif step[0] == "q":
            quant(T.ac, T.as_, T.ab, b, S["ld_a%d" % b], S["q_a%d" % b])
        elif step[0] == "m":
            vec.wait_ge(S["u%d" % b], 1)
            vec.tensor_scalar(T.mk[:, lo:hi], T.p[:, 512 * b:512 * b + 128], 0.0, 0.037, AluOpType.is_gt,
                              AluOpType.mult).then_inc(S["m%d" % b], 1)
        else:
            vec.wait_ge(S["d%d" % b], 1)
            vec.wait_ge(S["m%d" % b], 1)
            vec.tensor_tensor(T.t[:, b:512:4], T.p[:, 2048 + 512 * b:2048 + 512 * b + 128], T.mk[:, lo:hi],
                              AluOpType.mult).then_inc(S.r, 1)
    vec.wait_ge(S.r, 4)
    vec.quantize_mx(T.tc[:, W * own:W * own + W], T.ts[:, W * own:W * own + W], T.t[:]).then_inc(S.q_t, 1)
    quant(T.wc, T.ws, T.wb, 0, S.ld_w, S.q_w)
    quant(T.vc, T.vs, T.vb, 0, S.ld_v, S.q_v)

    for step in SCALAR:
        b = int(step[1])
        lo, hi = 128 * b, 128 * b + 128
        if step[0] == "s":
            g.scalar.wait_ge(S["u%d" % b], 1)
            g.scalar.activation(T.sg[:, lo:hi], T.p[:, 512 * b:512 * b + 128], ActivationFunctionType.Sign).then_inc(S["s%d" % b], 1)
        else:
            g.scalar.wait_ge(S["s%d" % b], 1)
            g.scalar.activation(T.mk[:, lo:hi], T.sg[:, lo:hi], ActivationFunctionType.Relu, scale=0.037).then_inc(S["m%d" % b], 1)

    for step in TENSOR:
        b = int(step[1])
        bank, c, s, first = (0, T.xc, T.xs, S.q_x) if step[0] == "u" else (4, T.ec, T.es, S.q_e)
        ten.wait_ge(first, 1)
        ten.wait_ge(S["q_a%d" % b], 1)
        ten.matmul_mx(T.p[:, 512 * (bank + b):512 * (bank + b) + 128], T.ac[:, W * b:W * b + W], T.as_[:, W * b:W * b + W],
                      c[:], s[:], True, True).then_inc(S[step], 1)

    count = {"sent": 0, "passed": 0}
    arrive = {("codes", "s", 0): (S.q_t, 1), ("plane", "s", 0): (S.q_t, 1)}

    def call(kind, routes, local):
        g.remote_dma_fused([RemoteDMATransfer(dst_ids=[dst(c) for c, _ in to], dma_engine_mask=m, remote_sem=sm,
                                              srcs=[view(kind, a, w)], dsts=[view(kind, q, w) for _, q in to])
                            for a, w, m, sm, to in routes], local_sem=S[local])
        count[local] += sum(bits(m) for _, _, m, _, _ in routes)

    g.wait_ge(S.q_t, 1)
    for kind, routes in SENDS:
        call(kind, [(own, 1, masks[m], sem(kind, core), [(at(*t), slot(t[1], me)) for t in to]) for m, to in routes], "sent")
        for m, to in routes:
            for side, k in to:
                arrive[(kind, side, k)] = (sem(kind, at(side, -k)), bits(masks[m]))
    for i, (kind, ks, m) in enumerate(FORWARDS):
        if i == STORE_AFTER:
            g.sem_inc(S.go, 1)
        for k in ks:
            g.wait_ge(*arrive[(kind, "s", k)])
            arrive[(kind, "o", k)] = (sem(kind, at("o", -ks[0])), bits(masks[m]))
        q = slot(ks[0], me)
        call(kind, [(q, len(ks), masks[m], sem(kind, at("s", -ks[0])), [(mate, q)])], "passed")

    for q in queues.values():
        q.wait_ge(S.go, 1)
    stores = {"sync": 0, "scalar": 0}
    z = T.p[:, 512 * BANKS:512 * BANKS + W]
    ten.wait_ge(S.q_w, 1)
    ten.wait_ge(S.q_v, 1)
    for i, ((side, k), queue) in enumerate(STEPS):
        maker = at(side, -k)
        r, a, bank = T.rank_of(maker), slot(k, place(maker)), 512 * (i % BANKS)
        codes, plane = T.tc[:, W * a:W * a + W], T.ts[:, W * a:W * a + W]
        ten.wait_ge(*arrive[("plane", side, k)])
        ten.wait_ge(*arrive[("codes", side, k)])
        if i >= BANKS:
            ten.wait_ge(S["y_cp%d" % (i - BANKS)], 1)
        ten.matmul_mx(T.p[:, bank:bank + W], T.wc[:], T.ws[:], codes, plane, True, True).then_inc(S["y_mm%d" % i], 1)
        mm = ten.matmul_mx(z, codes, plane, T.vc[:], T.vs[:], i == 0, i == len(STEPS) - 1)
        if i == len(STEPS) - 1:
            mm.then_inc(S.z_mm, 1)
        out, src = T.yo[:, W * r:W * r + W], T.p[:, bank:bank + W]
        if i in ON_SCALAR:
            g.scalar.wait_ge(S["y_mm%d" % i], 1)
            g.scalar.activation(out, src, ActivationFunctionType.Copy).then_inc(S["y_cp%d" % i], 1)
        else:
            vec.wait_ge(S["y_mm%d" % i], 1)
            vec.tensor_copy(out, src).then_inc(S["y_cp%d" % i], 1)
        if queue:
            queues[queue].wait_ge(S["y_cp%d" % i], 1)
            lo, hi = W * r, W * r + W
            if maker == mate:
                queues[queue].wait_ge(S.y_cp0, 1)
                lo = W * min(r, rank)
                hi = lo + 2 * W
            queues[queue].dma_start(T.y[:, lo:hi], T.yo[:, lo:hi]).then_inc(S["st_" + queue], 16)
            stores[queue] += 16
    g.scalar.wait_ge(S.z_mm, 1)
    g.scalar.activation(T.zo[:], z, ActivationFunctionType.Copy).then_inc(S.z_cp, 1)
    g.scalar.wait_ge(S.z_cp, 1)
    g.scalar.dma_start(T.z[:], T.zo[:]).then_inc(S.st_scalar, 16)
    for q in queues:
        queues[q].wait_ge(S["st_" + q], stores[q] + (16 if q == "scalar" else 0))
    g.wait_ge(S.sent, count["sent"])
    g.wait_ge(S.passed, count["passed"])
